import numpy as np
import ml_dtypes


def mxq(x, axis, fmt="e4m3"):
    dtype, down = {"e4m3": (ml_dtypes.float8_e4m3fn, 7), "e5m2": (ml_dtypes.float8_e5m2, 14)}[fmt]
    v = np.moveaxis(np.asarray(x, np.float32).astype(ml_dtypes.bfloat16).astype(np.float64), axis, -1)
    blocks = v.reshape(v.shape[:-1] + (-1, 32))
    amax = np.abs(blocks).max(-1, keepdims=True)
    byte = np.maximum(np.where(amax > 0, np.frexp(amax)[1] - 1 + 127, 0) - down, 1)
    scale = np.exp2(byte - 127.0)
    codes = (blocks / scale).astype(np.float32).astype(dtype).astype(np.float64)
    return np.moveaxis((codes * scale).reshape(v.shape), -1, axis)


WIDE = False


def mx_kscale(k):
    if not WIDE:
        return np.ones(k)
    levels = np.array([10, -10, 5, -5, 0])
    if k % 512:
        return np.exp2(np.random.permutation(np.resize(levels, k // 32))).repeat(32)
    a = np.empty((k // 512, 16))
    for p in range(k // 512):
        a[p, :8] = np.random.permutation(np.resize(levels, 8))
        for g in range(8):
            far = levels[np.abs(levels - a[p, g]) >= 10]
            a[p, g + 8] = far[np.random.randint(len(far))]
    return np.exp2(a.ravel()).repeat(32)


BF16 = ml_dtypes.bfloat16


def bf(x):
    return np.asarray(x, np.float32).astype(BF16)


def f64(x):
    return np.asarray(x).astype(np.float64)


M, N, R = 512, 6144, 512


def positive_part(t):
    return np.maximum(t, 0.0)


def negative_part(t):
    return np.maximum(-t, 0.0)


def draw0():
    s, t = mx_kscale(M), mx_kscale(R)
    return {"x": bf(np.random.standard_normal((M, N)) * 3.0 * s[:, None]),
            "f": bf(np.random.standard_normal((M, R)) * 1.5 / np.sqrt(M) * s[:, None]),
            "g": bf(np.random.uniform(0.1, 1.0, (N, R))),
            "m": bf(np.random.uniform(0.5, 1.5, M) / (s * s)),
            "c": bf(np.random.standard_normal(R) * t),
            "d": bf(np.random.uniform(0.25, 1.25, R) / (t * t))}


def core(x, f, g, m, c, d):
    x, f, g, m, c, d = f64(x), f64(f), f64(g), f64(m), f64(c), f64(d)
    fm = f * m[:, None]
    fmq = mxq(fm, 0, "e4m3")
    p = mxq(x, 0, "e4m3").T @ fmq
    a = mxq(f, 0, "e4m3").T @ fmq
    gcq = mxq(g * c[None, :], 1, "e4m3")
    e = c * d
    an = negative_part(a) * e[:, None]
    ap = positive_part(a) * e[:, None]
    gn = gcq @ mxq(an, 0, "e4m3")
    gp = gcq @ mxq(ap, 0, "e4m3")
    num = positive_part(p) + gn
    den = negative_part(p) + gp
    return g * np.sqrt(num / den)


def e4m3fn_bytes(y):
    return np.clip(np.asarray(y, np.float64), -448.0, 448.0).astype(np.float32).astype(ml_dtypes.float8_e4m3fn).view(np.uint8)


def e4m3fn_values(b):
    return np.asarray(b, np.uint8).view(ml_dtypes.float8_e4m3fn).astype(np.float64)


def setup_inputs():
    d = draw0()
    x0 = np.asarray(d['x']).astype(np.float64)
    s = (np.max(np.abs(x0), axis=(1,), keepdims=True) / 448.0).astype(np.float32)
    out = {}
    for k, v in d.items():
        if k == 'x':
            out['x_bytes'] = e4m3fn_bytes(x0 / s.astype(np.float64))
            out['x_scale'] = s
        else:
            out[k] = v
    return out


def reference(x_bytes, x_scale, f, g, m, c, d):
    return core(e4m3fn_values(x_bytes) * x_scale.astype(np.float64), f, g, m, c, d)

@@ -1,0 +1,311 @@
+from contextlib import ExitStack
+
+import concourse.mybir as mybir
+from concourse.masks import make_identity
+
+M, N, R = 512, 6144, 512
+FLOPS = 2 * (3 * N * M * R + M * R * R)
+
+P = 128
+T = 4
+ROWS = 2 * P
+STEPS = N // ROWS
+CHUNK = 2 * ROWS
+GROUPS = [4, 4, 4, 4, 4, 2, 2]
+
+F32 = mybir.dt.float32
+BF16 = mybir.dt.bfloat16
+U32 = mybir.dt.uint32
+U8 = mybir.dt.uint8
+FP8 = mybir.dt.float8_e4m3fn
+FP8X4 = mybir.dt.float8_e4m3fn_x4
+ALU = mybir.AluOpType
+ACT = mybir.ActivationFunctionType
+
+X_LOADS = [512, 512, 1024, 2048, 2048]
+G_LOADS = [1, 1, 2, 4, 4, 4, 4, 4]
+
+
+def plan():
+    order = []
+    first = 0
+    for index, size in enumerate(GROUPS):
+        names = ("sqrt", "rsqrt") if index % 2 == 0 else ("rsqrt", "sqrt")
+        for name in names:
+            for step in range(first, first + size):
+                order.append((name, step))
+        first += size
+    roots, products = [], []
+    seen = set()
+    position = 0
+    ready = []
+    sent = 0
+    for s in range(STEPS + 1):
+        count = len(ready) - sent if s == STEPS else min(len(ready) - sent, 1 if s < STEPS - 2 else 2)
+        products.append(ready[sent:sent + count])
+        sent += count
+        now = []
+        limit = 2 if s < STEPS else 2 * STEPS
+        while len(now) < limit and position < len(order) and order[position][1] < s:
+            name, step = order[position]
+            now.append((name, step))
+            if step in seen:
+                ready.append(step)
+            seen.add(step)
+            position += 1
+        roots.append(now)
+    products.append(ready[sent:])
+    return roots, products
+
+
+def tile_seminmfsquarerootupdate_t_kernel(tc, x_bytes, x_scale, f, g, m, c, d, out):
+    nc = tc.nc
+    with ExitStack() as ctx:
+        keep = ctx.enter_context(tc.tile_pool(name="keep", bufs=1))
+        work = ctx.enter_context(tc.tile_pool(name="work", bufs=2))
+        psum = ctx.enter_context(tc.psum_pool(name="psum", bufs=2))
+        ctx.enter_context(tc.manual_schedule())
+
+        f_raw = keep.tile([P, T, R], BF16, name="f_raw", tag="raw", bufs=2)
+        nc.sync.dma_start(out=f_raw[:], in_=f.rearrange("(p t) r -> p t r", t=T))
+        m_col = keep.tile([P, T], BF16, name="m_col")
+        nc.scalar.dma_start(out=m_col[:], in_=m.rearrange("(p t) -> p t", t=T))
+        xs_col = keep.tile([P, T], F32, name="xs_col")
+        nc.scalar.dma_start(out=xs_col[:], in_=x_scale.rearrange("(p t) o -> p (t o)", t=T))
+        c_col = keep.tile([P, T], BF16, name="c_col")
+        nc.scalar.dma_start(out=c_col[:], in_=c.rearrange("(p t) -> p t", t=T))
+        d_col = keep.tile([P, T], BF16, name="d_col")
+        nc.scalar.dma_start(out=d_col[:], in_=d.rearrange("(p t) -> p t", t=T))
+
+        xb = x_bytes.rearrange("(p t) n -> p t n", t=T)
+        x_codes = {}
+        g_rows = {}
+
+        def load_x(index):
+            first = sum(X_LOADS[:index])
+            width = X_LOADS[index]
+            t = keep.tile([P, T, width], U8, name="x_in%d" % index)
+            nc.sync.dma_start(out=t[:], in_=xb[:, :, first:first + width])
+            for k in range(width // CHUNK):
+                x_codes[first // CHUNK + k] = (t, k * CHUNK)
+
+        def load_g(index):
+            first = sum(G_LOADS[:index])
+            steps = G_LOADS[index]
+            t = keep.tile([P, 2 * steps, R], BF16, name="g_in%d" % index)
+            rows = g[first * ROWS:(first + steps) * ROWS, :]
+            nc.sync.dma_start(out=t[:], in_=rows.rearrange("(i p) r -> p i r", p=P))
+            for k in range(steps):
+                g_rows[first + k] = (t, 2 * k)
+
+        load_x(0)
+        load_g(0)
+        load_g(1)
+        load_x(1)
+        load_g(2)
+        load_x(2)
+        load_g(3)
+        load_x(3)
+        load_g(4)
+        load_g(5)
+        load_x(4)
+        load_g(6)
+        load_g(7)
+
+        ident = keep.tile([P, P], F32, name="ident")
+        make_identity(nc, ident[:])
+
+        xw, xi, xq, xsc = {}, {}, {}, {}
+        gt, gi, gq, gsc = {}, {}, {}, {}
+        pp, pc, nn, dd = {}, {}, {}, {}
+        num, den = {}, {}
+
+        def widen(k, ts):
+            if k not in xw:
+                xw[k] = work.tile([P, T, CHUNK], BF16, name="xw", tag="xw", bufs=3)
+            src, first = x_codes[k]
+            for t in ts:
+                nc.scalar.activation(
+                    xw[k][:, t, :], src[:, t, first:first + CHUNK].bitcast(FP8), ACT.Copy,
+                    scale=xs_col[:, t:t + 1])
+
+        def x_interleave(s):
+            src = xw[s // 2][:, :, (s % 2) * ROWS:(s % 2 + 1) * ROWS]
+            xi[s] = work.tile([P, ROWS, T], BF16, name="xi", tag="xi", bufs=2, align_bytes=64)
+            nc.vector.tensor_copy(
+                out=xi[s][:].rearrange("p (b i) t -> p b t i", i=4),
+                in_=src.rearrange("p t (b i) -> p b t i", i=4))
+
+        def x_quantise(s):
+            xq[s] = work.tile([P, ROWS], U32, name="xq", tag="xq", bufs=3, align_bytes=64)
+            xsc[s] = work.tile([P, ROWS], U8, name="xsc", tag="xsc", bufs=3, align_bytes=64)
+            nc.vector.quantize_mx(out=xq[s][:].bitcast(FP8X4), scales=xsc[s][:],
+                                  in_=xi[s][:].rearrange("p n t -> p (n t)"))
+
+        def g_transpose(s):
+            src, first = g_rows[s]
+            gt[s] = psum.tile([P, 2, ROWS], F32, name="gt", tag="gt", bufs=2)
+            for u in range(2):
+                for i in range(2):
+                    words = src[:, first + i, :].bitcast(F32)
+                    nc.tensor.transpose(gt[s][:, u, i * P:(i + 1) * P], words[:, u::2], ident[:])
+
+        def g_scale(s):
+            gi[s] = work.tile([P, ROWS, T], BF16, name="gi", tag="gi", bufs=2, align_bytes=64)
+            nc.vector.tensor_tensor(
+                out=gi[s][:].rearrange("p n (u e) -> p n u e", e=2),
+                in0=gt[s][:].bitcast(BF16).rearrange("p u (n e) -> p n u e", e=2),
+                in1=c_col[:].rearrange("p (u e) -> p u e", e=2).unsqueeze(1).to_broadcast([P, ROWS, 2, 2]),
+                op=ALU.mult)
+
+        def g_quantise(s):
+            gq[s] = work.tile([P, ROWS], U32, name="gq", tag="gq", bufs=4, align_bytes=64)
+            gsc[s] = work.tile([P, ROWS], U8, name="gsc", tag="gsc", bufs=4, align_bytes=64)
+            nc.vector.quantize_mx(out=gq[s][:].bitcast(FP8X4), scales=gsc[s][:],
+                                  in_=gi[s][:].rearrange("p n t -> p (n t)"))
+
+        def mm(dst, codes, scales, i, moving):
+            nc.tensor.matmul_mx(
+                out=dst, lhsT=codes[:, i * P:(i + 1) * P].bitcast(FP8X4),
+                lhsT_scale=scales[:, i * P:(i + 1) * P],
+                rhs=moving[0][:].bitcast(FP8X4), rhs_scale=moving[1][:], start=True, stop=True)
+
+        def p_matmul(s):
+            for i in range(2):
+                pp[s, i] = psum.tile([P, R], F32, name="pp", tag="pp", bufs=2)
+                mm(pp[s, i][:], xq[s], xsc[s], i, fmq)
+
+        def p_copy(s):
+            for i in range(2):
+                pc[s, i] = work.tile([P, R], F32, name="pc", tag="pc", bufs=4)
+                nc.scalar.copy(out=pc[s, i][:], in_=pp[s, i][:])
+
+        def g_matmul(s):
+            for i in range(2):
+                nn[s, i] = psum.tile([P, R], F32, name="nn", tag="nn", bufs=2)
+                mm(nn[s, i][:], gq[s], gsc[s], i, anq)
+                dd[s, i] = psum.tile([P, R], F32, name="dd", tag="dd", bufs=2)
+                mm(dd[s, i][:], gq[s], gsc[s], i, apq)
+
+        def ratio_parts(s):
+            num[s] = work.tile([P, 2, R], F32, name="num", tag="num", bufs=9)
+            den[s] = work.tile([P, 2, R], F32, name="den", tag="den", bufs=9)
+            for i in range(2):
+                nc.vector.scalar_tensor_tensor(
+                    out=num[s][:, i, :], in0=pc[s, i][:], scalar=0.0, in1=nn[s, i][:], op0=ALU.max, op1=ALU.add)
+                nc.vector.scalar_tensor_tensor(
+                    out=den[s][:, i, :], in0=pc[s, i][:], scalar=0.0, in1=dd[s, i][:], op0=ALU.min, op1=ALU.subtract)
+
+        def root(name, s):
+            if name == "sqrt":
+                nc.scalar.activation(num[s][:], num[s][:], ACT.Sqrt)
+            else:
+                nc.scalar.activation(den[s][:], den[s][:], ACT.Abs_reciprocal_sqrt, scale=-1.0)
+
+        def product(s):
+            nc.vector.tensor_tensor(out=num[s][:], in0=num[s][:], in1=den[s][:], op=ALU.mult)
+
+        def finish(s):
+            src, first = g_rows[s]
+            res = work.tile([P, 2, R], F32, name="res", tag="res", bufs=3)
+            eng = nc.gpsimd if s < STEPS - 3 else nc.vector
+            eng.tensor_tensor(out=res[:], in0=num[s][:], in1=src[:, first:first + 2, :], op=ALU.mult)
+            nc.sync.dma_start(out=out[s * ROWS:(s + 1) * ROWS, :].rearrange("(i p) r -> p i r", p=P), in_=res[:])
+
+        fm_raw = keep.tile([P, T, R], BF16, name="fm_raw", tag="raw", bufs=2)
+        for t in range(T):
+            nc.vector.tensor_scalar(out=fm_raw[:, t, :], in0=f_raw[:, t, :], scalar1=m_col[:, t:t + 1],
+                                    scalar2=None, op0=ALU.mult)
+        fi = keep.tile([P, R, T], BF16, name="fi", tag="il", bufs=2, align_bytes=64)
+        nc.scalar.copy(out=fi[:].rearrange("p (q w) t -> p q w t", q=T),
+                       in_=f_raw[:].rearrange("p t (w q) -> p q w t", q=T))
+        fmi = keep.tile([P, R, T], BF16, name="fmi", tag="il", bufs=2, align_bytes=64)
+        nc.vector.tensor_copy(out=fmi[:].rearrange("p (b i) t -> p b t i", i=4),
+                              in_=fm_raw[:].rearrange("p t (b i) -> p b t i", i=4))
+        e_col = keep.tile([P, T], F32, name="e_col")
+        nc.vector.tensor_tensor(out=e_col[:], in0=c_col[:], in1=d_col[:], op=ALU.mult)
+        ne_col = keep.tile([P, T], F32, name="ne_col")
+        nc.vector.tensor_scalar(out=ne_col[:], in0=e_col[:], scalar1=-1.0, scalar2=None, op0=ALU.mult)
+
+        def quantised(src, label):
+            codes = keep.tile([P, R], U32, name=label + "_codes", align_bytes=64)
+            scales = keep.tile([P, R], U8, name=label + "_scales", align_bytes=64)
+            nc.vector.quantize_mx(out=codes[:].bitcast(FP8X4), scales=scales[:],
+                                  in_=src[:].rearrange("p n t -> p (n t)"))
+            return codes, scales
+
+        fmq = quantised(fmi, "fm")
+        fq = quantised(fi, "f")
+        a_tags = ("nn", "dd", "nn", "dd")
+        a_bank = []
+        for q in range(T):
+            t = psum.tile([P, R], F32, name="a%d" % q, tag=a_tags[q], bufs=2)
+            mm(t[:], fq[0], fq[1], q, fmq)
+            a_bank.append(t)
+
+        widen(0, range(T))
+        g_transpose(0)
+        g_transpose(1)
+        x_interleave(0)
+        g_scale(0)
+        x_quantise(0)
+        g_quantise(0)
+        p_matmul(0)
+        p_copy(0)
+
+        an_raw = keep.tile([P, T, R], BF16, name="an_raw", tag="raw", bufs=2)
+        ap_raw = keep.tile([P, T, R], BF16, name="ap_raw", tag="raw", bufs=2)
+        an_i = keep.tile([P, R, T], BF16, name="an_i", tag="il", bufs=2, align_bytes=64)
+        ap_i = keep.tile([P, R, T], BF16, name="ap_i", tag="il", bufs=2, align_bytes=64)
+        for q in range(T):
+            nc.vector.tensor_scalar(out=an_raw[:, q, :], in0=a_bank[q][:], scalar1=0.0, scalar2=ne_col[:, q:q + 1],
+                                    op0=ALU.min, op1=ALU.mult)
+        nc.scalar.copy(out=an_i[:].rearrange("p (b i) t -> p b t i", i=4),
+                       in_=an_raw[:].rearrange("p t (b i) -> p b t i", i=4))
+        for q in range(T):
+            nc.vector.tensor_scalar(out=ap_raw[:, q, :], in0=a_bank[q][:], scalar1=0.0, scalar2=e_col[:, q:q + 1],
+                                    op0=ALU.max, op1=ALU.mult)
+        widen(1, range(T))
+        x_interleave(1)
+        nc.vector.tensor_copy(out=ap_i[:].rearrange("p (b i) t -> p b t i", i=4),
+                              in_=ap_raw[:].rearrange("p t (b i) -> p b t i", i=4))
+        anq = quantised(an_i, "an")
+        x_quantise(1)
+        apq = quantised(ap_i, "ap")
+        g_scale(1)
+        g_transpose(2)
+        g_quantise(1)
+
+        roots, products = plan()
+        for s in range(STEPS):
+            g_matmul(s)
+            if s + 1 < STEPS:
+                p_matmul(s + 1)
+            if s + 3 < STEPS:
+                g_transpose(s + 3)
+            for name, w in roots[s][:1]:
+                root(name, w)
+            if s + 1 < STEPS:
+                p_copy(s + 1)
+            for name, w in roots[s][1:]:
+                root(name, w)
+            ratio_parts(s)
+            if s + 2 < STEPS:
+                g_scale(s + 2)
+                x_interleave(s + 2)
+                g_quantise(s + 2)
+                x_quantise(s + 2)
+            k = (s + 4) // 2
+            if k < STEPS // 2:
+                widen(k, (0, 1) if s % 2 == 0 else (2, 3))
+            for w in products[s]:
+                product(w)
+                finish(w)
+        for w in products[STEPS]:
+            product(w)
+            finish(w)
+        for name, w in roots[STEPS]:
+            root(name, w)
+        for w in products[STEPS + 1]:
+            product(w)
+            finish(w)

@@ -11,7 +11,17 @@ T = 4
 ROWS = 2 * P
 STEPS = N // ROWS
 CHUNK = 2 * ROWS
-GROUPS = [4, 4, 4, 4, 4, 2, 2]
+BLOCKS = N // CHUNK
+GROUPS = [2, 4, 4, 4, 4, 4, 2]
+S_INT = ()
+G_INT = (2, 3)
+TAIL_V = 1
+ACT_RATE = (2, 3)
+ACT_LATE = 18
+LATE = 22
+G_FIN = 2
+NBUF = 9
+G_HALF = False
 
 F32 = mybir.dt.float32
 BF16 = mybir.dt.bfloat16
@@ -23,7 +33,7 @@ ALU = mybir.AluOpType
 ACT = mybir.ActivationFunctionType
 
 X_LOADS = [512, 512, 1024, 2048, 2048]
-G_LOADS = [1, 1, 2, 4, 4, 4, 4, 4]
+G_LOADS = [1, 1, 1, 1, 2, 2, 2, 2]
 
 
 def plan():
@@ -40,13 +50,12 @@ def plan():
     position = 0
     ready = []
     sent = 0
-    for s in range(STEPS + 1):
-        count = len(ready) - sent if s == STEPS else min(len(ready) - sent, 1 if s < STEPS - 2 else 2)
+    for s in range(STEPS):
+        count = min(len(ready) - sent, 1 if s < LATE else 2)
         products.append(ready[sent:sent + count])
         sent += count
         now = []
-        limit = 2 if s < STEPS else 2 * STEPS
-        while len(now) < limit and position < len(order) and order[position][1] < s:
+        while len(now) < ACT_RATE[s >= ACT_LATE] and position < len(order) and order[position][1] < s:
             name, step = order[position]
             now.append((name, step))
             if step in seen:
@@ -54,8 +63,7 @@ def plan():
             seen.add(step)
             position += 1
         roots.append(now)
-    products.append(ready[sent:])
-    return roots, products
+    return roots, products, order[position:]
 
 
 def tile_seminmfsquarerootupdate_t_kernel(tc, x_bytes, x_scale, f, g, m, c, d, out):
@@ -66,8 +74,10 @@ def tile_seminmfsquarerootupdate_t_kernel(tc, x_bytes, x_scale, f, g, m, c, d, o
         psum = ctx.enter_context(tc.psum_pool(name="psum", bufs=2))
         ctx.enter_context(tc.manual_schedule())
 
-        f_raw = keep.tile([P, T, R], BF16, name="f_raw", tag="raw", bufs=2)
-        nc.sync.dma_start(out=f_raw[:], in_=f.rearrange("(p t) r -> p t r", t=T))
+        f_raw = work.tile([P, T, R], BF16, name="f_raw", tag="raw", bufs=3)
+        f_rows = f.rearrange("(p t) r -> p t r", t=T)
+        nc.sync.dma_start(out=f_raw[:, 0:2, :], in_=f_rows[:, 0:2, :])
+        nc.sync.dma_start(out=f_raw[:, 2:4, :], in_=f_rows[:, 2:4, :])
         m_col = keep.tile([P, T], BF16, name="m_col")
         nc.scalar.dma_start(out=m_col[:], in_=m.rearrange("(p t) -> p t", t=T))
         xs_col = keep.tile([P, T], F32, name="xs_col")
@@ -78,8 +88,8 @@ def tile_seminmfsquarerootupdate_t_kernel(tc, x_bytes, x_scale, f, g, m, c, d, o
         nc.scalar.dma_start(out=d_col[:], in_=d.rearrange("(p t) -> p t", t=T))
 
         xb = x_bytes.rearrange("(p t) n -> p t n", t=T)
-        x_codes = {}
-        g_rows = {}
+        x_in = {}
+        g_in = {}
 
         def load_x(index):
             first = sum(X_LOADS[:index])
@@ -87,23 +97,22 @@ def tile_seminmfsquarerootupdate_t_kernel(tc, x_bytes, x_scale, f, g, m, c, d, o
             t = keep.tile([P, T, width], U8, name="x_in%d" % index)
             nc.sync.dma_start(out=t[:], in_=xb[:, :, first:first + width])
             for k in range(width // CHUNK):
-                x_codes[first // CHUNK + k] = (t, k * CHUNK)
+                x_in[first // CHUNK + k] = (t, k * CHUNK)
 
         def load_g(index):
-            first = sum(G_LOADS[:index])
-            steps = G_LOADS[index]
-            t = keep.tile([P, 2 * steps, R], BF16, name="g_in%d" % index)
-            rows = g[first * ROWS:(first + steps) * ROWS, :]
-            nc.sync.dma_start(out=t[:], in_=rows.rearrange("(i p) r -> p i r", p=P))
-            for k in range(steps):
-                g_rows[first + k] = (t, 2 * k)
+            first = sum(G_LOADS[:index]) * CHUNK
+            tiles = G_LOADS[index] * CHUNK // P
+            t = keep.tile([P, tiles, R], BF16, name="g_in%d" % index)
+            nc.sync.dma_start(out=t[:], in_=g[first:first + tiles * P, :].rearrange("(i p) r -> p i r", p=P))
+            for k in range(tiles // 2):
+                g_in[first // ROWS + k] = (t, 2 * k)
 
         load_x(0)
         load_g(0)
-        load_g(1)
         load_x(1)
-        load_g(2)
+        load_g(1)
         load_x(2)
+        load_g(2)
         load_g(3)
         load_x(3)
         load_g(4)
@@ -115,35 +124,32 @@ def tile_seminmfsquarerootupdate_t_kernel(tc, x_bytes, x_scale, f, g, m, c, d, o
         ident = keep.tile([P, P], F32, name="ident")
         make_identity(nc, ident[:])
 
-        xw, xi, xq, xsc = {}, {}, {}, {}
-        gt, gi, gq, gsc = {}, {}, {}, {}
+        xw, xi, xt, xq = {}, {}, {}, {}
+        gt, gi, gq = {}, {}, {}
         pp, pc, nn, dd = {}, {}, {}, {}
         num, den = {}, {}
 
-        def widen(k, ts):
+        def widen(k, planes):
             if k not in xw:
-                xw[k] = work.tile([P, T, CHUNK], BF16, name="xw", tag="xw", bufs=3)
-            src, first = x_codes[k]
-            for t in ts:
-                nc.scalar.activation(
-                    xw[k][:, t, :], src[:, t, first:first + CHUNK].bitcast(FP8), ACT.Copy,
-                    scale=xs_col[:, t:t + 1])
+                xw[k] = work.tile([P, T, CHUNK], BF16, name="xw", tag="raw", bufs=3)
+            src, first = x_in[k]
+            for t in planes:
+                nc.scalar.activation(xw[k][:, t, :], src[:, t, first:first + CHUNK].bitcast(FP8), ACT.Copy,
+                                     scale=xs_col[:, t:t + 1])
 
-        def x_interleave(s):
-            src = xw[s // 2][:, :, (s % 2) * ROWS:(s % 2 + 1) * ROWS]
-            xi[s] = work.tile([P, ROWS, T], BF16, name="xi", tag="xi", bufs=2, align_bytes=64)
-            nc.vector.tensor_copy(
-                out=xi[s][:].rearrange("p (b i) t -> p b t i", i=4),
-                in_=src.rearrange("p t (b i) -> p b t i", i=4))
+        def x_interleave(k):
+            xi[k] = work.tile([P, CHUNK, T], BF16, name="xi", tag="xi", bufs=3, align_bytes=64)
+            if k in G_INT:
+                nc.gpsimd.tensor_scalar(out=xi[k][:].rearrange("p (b i) t -> p b t i", i=4),
+                                        in0=xw[k][:].rearrange("p t (b i) -> p b t i", i=4),
+                                        scalar1=1.0, scalar2=0.0, op0=ALU.mult, op1=ALU.add)
+                return
+            engine = nc.scalar.copy if k in S_INT else nc.vector.tensor_copy
+            engine(out=xi[k][:].rearrange("p (b i) t -> p b t i", i=4),
+                   in_=xw[k][:].rearrange("p t (b i) -> p b t i", i=4))
 
-        def x_quantise(s):
-            xq[s] = work.tile([P, ROWS], U32, name="xq", tag="xq", bufs=3, align_bytes=64)
-            xsc[s] = work.tile([P, ROWS], U8, name="xsc", tag="xsc", bufs=3, align_bytes=64)
-            nc.vector.quantize_mx(out=xq[s][:].bitcast(FP8X4), scales=xsc[s][:],
-                                  in_=xi[s][:].rearrange("p n t -> p (n t)"))
-
-        def g_transpose(s):
-            src, first = g_rows[s]
+        def g_turn(s):
+            src, first = g_in[s]
             gt[s] = psum.tile([P, 2, ROWS], F32, name="gt", tag="gt", bufs=2)
             for u in range(2):
                 for i in range(2):
@@ -151,50 +157,57 @@ def tile_seminmfsquarerootupdate_t_kernel(tc, x_bytes, x_scale, f, g, m, c, d, o
                     nc.tensor.transpose(gt[s][:, u, i * P:(i + 1) * P], words[:, u::2], ident[:])
 
         def g_scale(s):
-            gi[s] = work.tile([P, ROWS, T], BF16, name="gi", tag="gi", bufs=2, align_bytes=64)
+            k, h = s // 2, s % 2
+            if h == 0:
+                gi[k] = work.tile([P, CHUNK, T], BF16, name="gi", tag="il", bufs=3, align_bytes=64)
             nc.vector.tensor_tensor(
-                out=gi[s][:].rearrange("p n (u e) -> p n u e", e=2),
+                out=gi[k][:, h * ROWS:(h + 1) * ROWS, :].rearrange("p n (u e) -> p n u e", e=2),
                 in0=gt[s][:].bitcast(BF16).rearrange("p u (n e) -> p n u e", e=2),
                 in1=c_col[:].rearrange("p (u e) -> p u e", e=2).unsqueeze(1).to_broadcast([P, ROWS, 2, 2]),
                 op=ALU.mult)
 
-        def g_quantise(s):
-            gq[s] = work.tile([P, ROWS], U32, name="gq", tag="gq", bufs=4, align_bytes=64)
-            gsc[s] = work.tile([P, ROWS], U8, name="gsc", tag="gsc", bufs=4, align_bytes=64)
-            nc.vector.quantize_mx(out=gq[s][:].bitcast(FP8X4), scales=gsc[s][:],
-                                  in_=gi[s][:].rearrange("p n t -> p (n t)"))
+        def quantised(src, pool, tag, bufs):
+            codes = pool.tile([P, CHUNK], U32, name=tag + "_codes", tag=tag + "_codes", bufs=bufs, align_bytes=64)
+            scales = pool.tile([P, CHUNK], U8, name=tag + "_scales", tag=tag + "_scales", bufs=bufs, align_bytes=64)
+            nc.vector.quantize_mx(out=codes[:].bitcast(FP8X4), scales=scales[:],
+                                  in_=src[:].rearrange("p n t -> p (n t)"))
+            return codes, scales
 
-        def mm(dst, codes, scales, i, moving):
+        def x_quantise(k):
+            xq[k] = quantised(xi[k], work, "xq", 3)
+
+        def g_quantise(k):
+            gq[k] = quantised(gi[k], work, "gq", 3)
+
+        def mm(dst, stationary, first, moving):
             nc.tensor.matmul_mx(
-                out=dst, lhsT=codes[:, i * P:(i + 1) * P].bitcast(FP8X4),
-                lhsT_scale=scales[:, i * P:(i + 1) * P],
+                out=dst, lhsT=stationary[0][:, first:first + P].bitcast(FP8X4),
+                lhsT_scale=stationary[1][:, first:first + P],
                 rhs=moving[0][:].bitcast(FP8X4), rhs_scale=moving[1][:], start=True, stop=True)
 
-        def p_matmul(s):
-            for i in range(2):
-                pp[s, i] = psum.tile([P, R], F32, name="pp", tag="pp", bufs=2)
-                mm(pp[s, i][:], xq[s], xsc[s], i, fmq)
+        def p_matmul(j):
+            pp[j] = psum.tile([P, R], F32, name="pp", tag="pp", bufs=2)
+            mm(pp[j][:], xq[j // 4], (j % 4) * P, fmq)
 
-        def p_copy(s):
-            for i in range(2):
-                pc[s, i] = work.tile([P, R], F32, name="pc", tag="pc", bufs=4)
-                nc.scalar.copy(out=pc[s, i][:], in_=pp[s, i][:])
+        def p_copy(j):
+            pc[j] = work.tile([P, R], F32, name="pc", tag="pc", bufs=8)
+            nc.scalar.copy(out=pc[j][:], in_=pp[j][:])
 
-        def g_matmul(s):
-            for i in range(2):
-                nn[s, i] = psum.tile([P, R], F32, name="nn", tag="nn", bufs=2)
-                mm(nn[s, i][:], gq[s], gsc[s], i, anq)
-                dd[s, i] = psum.tile([P, R], F32, name="dd", tag="dd", bufs=2)
-                mm(dd[s, i][:], gq[s], gsc[s], i, apq)
+        def g_matmul(j):
+            nn[j] = psum.tile([P, R], F32, name="nn", tag="nn", bufs=2)
+            mm(nn[j][:], gq[j // 4], (j % 4) * P, anq)
+            dd[j] = psum.tile([P, R], F32, name="dd", tag="dd", bufs=2)
+            mm(dd[j][:], gq[j // 4], (j % 4) * P, apq)
 
-        def ratio_parts(s):
-            num[s] = work.tile([P, 2, R], F32, name="num", tag="num", bufs=9)
-            den[s] = work.tile([P, 2, R], F32, name="den", tag="den", bufs=9)
-            for i in range(2):
-                nc.vector.scalar_tensor_tensor(
-                    out=num[s][:, i, :], in0=pc[s, i][:], scalar=0.0, in1=nn[s, i][:], op0=ALU.max, op1=ALU.add)
-                nc.vector.scalar_tensor_tensor(
-                    out=den[s][:, i, :], in0=pc[s, i][:], scalar=0.0, in1=dd[s, i][:], op0=ALU.min, op1=ALU.subtract)
+        def ratio_parts(j):
+            s, i = j // 2, j % 2
+            if i == 0:
+                num[s] = work.tile([P, 2, R], F32, name="num", tag="num", bufs=NBUF)
+                den[s] = work.tile([P, 2, R], F32, name="den", tag="den", bufs=NBUF)
+            nc.vector.scalar_tensor_tensor(
+                out=num[s][:, i, :], in0=pc[j][:], scalar=0.0, in1=nn[j][:], op0=ALU.max, op1=ALU.add)
+            nc.vector.scalar_tensor_tensor(
+                out=den[s][:, i, :], in0=pc[j][:], scalar=0.0, in1=dd[j][:], op0=ALU.min, op1=ALU.subtract)
 
         def root(name, s):
             if name == "sqrt":
@@ -202,24 +215,24 @@ def tile_seminmfsquarerootupdate_t_kernel(tc, x_bytes, x_scale, f, g, m, c, d, o
             else:
                 nc.scalar.activation(den[s][:], den[s][:], ACT.Abs_reciprocal_sqrt, scale=-1.0)
 
-        def product(s):
-            nc.vector.tensor_tensor(out=num[s][:], in0=num[s][:], in1=den[s][:], op=ALU.mult)
+        def product(engine, s, first=0, last=2):
+            engine.tensor_tensor(out=num[s][:, first:last, :], in0=num[s][:, first:last, :],
+                                 in1=den[s][:, first:last, :], op=ALU.mult)
 
-        def finish(s):
-            src, first = g_rows[s]
+        def finish(engine, s):
+            src, first = g_in[s]
             res = work.tile([P, 2, R], F32, name="res", tag="res", bufs=3)
-            eng = nc.gpsimd if s < STEPS - 3 else nc.vector
-            eng.tensor_tensor(out=res[:], in0=num[s][:], in1=src[:, first:first + 2, :], op=ALU.mult)
+            engine.tensor_tensor(out=res[:], in0=num[s][:], in1=src[:, first:first + 2, :], op=ALU.mult)
             nc.sync.dma_start(out=out[s * ROWS:(s + 1) * ROWS, :].rearrange("(i p) r -> p i r", p=P), in_=res[:])
 
-        fm_raw = keep.tile([P, T, R], BF16, name="fm_raw", tag="raw", bufs=2)
+        fm_raw = work.tile([P, T, R], BF16, name="fm_raw", tag="raw", bufs=3)
         for t in range(T):
             nc.vector.tensor_scalar(out=fm_raw[:, t, :], in0=f_raw[:, t, :], scalar1=m_col[:, t:t + 1],
                                     scalar2=None, op0=ALU.mult)
-        fi = keep.tile([P, R, T], BF16, name="fi", tag="il", bufs=2, align_bytes=64)
+        fi = work.tile([P, R, T], BF16, name="fi", tag="il", bufs=3, align_bytes=64)
         nc.scalar.copy(out=fi[:].rearrange("p (q w) t -> p q w t", q=T),
                        in_=f_raw[:].rearrange("p t (w q) -> p q w t", q=T))
-        fmi = keep.tile([P, R, T], BF16, name="fmi", tag="il", bufs=2, align_bytes=64)
+        fmi = work.tile([P, R, T], BF16, name="fmi", tag="il", bufs=3, align_bytes=64)
         nc.vector.tensor_copy(out=fmi[:].rearrange("p (b i) t -> p b t i", i=4),
                               in_=fm_raw[:].rearrange("p t (b i) -> p b t i", i=4))
         e_col = keep.tile([P, T], F32, name="e_col")
@@ -227,85 +240,87 @@ def tile_seminmfsquarerootupdate_t_kernel(tc, x_bytes, x_scale, f, g, m, c, d, o
         ne_col = keep.tile([P, T], F32, name="ne_col")
         nc.vector.tensor_scalar(out=ne_col[:], in0=e_col[:], scalar1=-1.0, scalar2=None, op0=ALU.mult)
 
-        def quantised(src, label):
-            codes = keep.tile([P, R], U32, name=label + "_codes", align_bytes=64)
-            scales = keep.tile([P, R], U8, name=label + "_scales", align_bytes=64)
-            nc.vector.quantize_mx(out=codes[:].bitcast(FP8X4), scales=scales[:],
-                                  in_=src[:].rearrange("p n t -> p (n t)"))
-            return codes, scales
-
-        fmq = quantised(fmi, "fm")
-        fq = quantised(fi, "f")
+        g_turn(0)
+        g_turn(1)
+        g_scale(0)
+        fmq = quantised(fmi, keep, "fm", 1)
+        fq = quantised(fi, keep, "f", 1)
         a_tags = ("nn", "dd", "nn", "dd")
         a_bank = []
         for q in range(T):
             t = psum.tile([P, R], F32, name="a%d" % q, tag=a_tags[q], bufs=2)
-            mm(t[:], fq[0], fq[1], q, fmq)
+            mm(t[:], fq, q * P, fmq)
             a_bank.append(t)
-
+        g_scale(1)
+        g_turn(2)
         widen(0, range(T))
-        g_transpose(0)
-        g_transpose(1)
         x_interleave(0)
-        g_scale(0)
-        x_quantise(0)
         g_quantise(0)
-        p_matmul(0)
-        p_copy(0)
-
-        an_raw = keep.tile([P, T, R], BF16, name="an_raw", tag="raw", bufs=2)
-        ap_raw = keep.tile([P, T, R], BF16, name="ap_raw", tag="raw", bufs=2)
-        an_i = keep.tile([P, R, T], BF16, name="an_i", tag="il", bufs=2, align_bytes=64)
-        ap_i = keep.tile([P, R, T], BF16, name="ap_i", tag="il", bufs=2, align_bytes=64)
+        a_sb = [work.tile([P, 2, R], F32, name="a_sb%d" % h, tag="num", bufs=NBUF) for h in range(2)]
         for q in range(T):
-            nc.vector.tensor_scalar(out=an_raw[:, q, :], in0=a_bank[q][:], scalar1=0.0, scalar2=ne_col[:, q:q + 1],
-                                    op0=ALU.min, op1=ALU.mult)
+            nc.scalar.copy(out=a_sb[q // 2][:, q % 2, :], in_=a_bank[q][:])
+        x_quantise(0)
+        widen(1, range(T))
+        an_raw = work.tile([P, T, R], BF16, name="an_raw", tag="raw", bufs=3)
+        for q in range(T):
+            nc.vector.tensor_scalar(out=an_raw[:, q, :], in0=a_sb[q // 2][:, q % 2, :], scalar1=0.0,
+                                    scalar2=ne_col[:, q:q + 1], op0=ALU.min, op1=ALU.mult)
+        an_i = work.tile([P, R, T], BF16, name="an_i", tag="il", bufs=3, align_bytes=64)
         nc.scalar.copy(out=an_i[:].rearrange("p (b i) t -> p b t i", i=4),
                        in_=an_raw[:].rearrange("p t (b i) -> p b t i", i=4))
+        ap_raw = work.tile([P, T, R], BF16, name="ap_raw", tag="raw", bufs=3)
         for q in range(T):
-            nc.vector.tensor_scalar(out=ap_raw[:, q, :], in0=a_bank[q][:], scalar1=0.0, scalar2=e_col[:, q:q + 1],
-                                    op0=ALU.max, op1=ALU.mult)
-        widen(1, range(T))
+            nc.vector.tensor_scalar(out=ap_raw[:, q, :], in0=a_sb[q // 2][:, q % 2, :], scalar1=0.0,
+                                    scalar2=e_col[:, q:q + 1], op0=ALU.max, op1=ALU.mult)
         x_interleave(1)
+        for j in range(2):
+            p_matmul(j)
+            p_copy(j)
+        ap_i = work.tile([P, R, T], BF16, name="ap_i", tag="il", bufs=3, align_bytes=64)
         nc.vector.tensor_copy(out=ap_i[:].rearrange("p (b i) t -> p b t i", i=4),
                               in_=ap_raw[:].rearrange("p t (b i) -> p b t i", i=4))
-        anq = quantised(an_i, "an")
+        anq = quantised(an_i, keep, "an", 1)
         x_quantise(1)
-        apq = quantised(ap_i, "ap")
-        g_scale(1)
-        g_transpose(2)
-        g_quantise(1)
+        apq = quantised(ap_i, keep, "ap", 1)
+        widen(2, range(T))
 
-        roots, products = plan()
+        roots, products, last_roots = plan()
         for s in range(STEPS):
-            g_matmul(s)
+            c, odd = s // 2, s % 2
+            g_matmul(2 * s)
+            g_matmul(2 * s + 1)
             if s + 1 < STEPS:
-                p_matmul(s + 1)
+                p_matmul(2 * s + 2)
+                p_matmul(2 * s + 3)
             if s + 3 < STEPS:
-                g_transpose(s + 3)
+                g_turn(s + 3)
             for name, w in roots[s][:1]:
                 root(name, w)
             if s + 1 < STEPS:
-                p_copy(s + 1)
+                p_copy(2 * s + 2)
+                p_copy(2 * s + 3)
             for name, w in roots[s][1:]:
                 root(name, w)
-            ratio_parts(s)
+            ratio_parts(2 * s)
+            ratio_parts(2 * s + 1)
             if s + 2 < STEPS:
                 g_scale(s + 2)
-                x_interleave(s + 2)
-                g_quantise(s + 2)
-                x_quantise(s + 2)
-            k = (s + 4) // 2
-            if k < STEPS // 2:
-                widen(k, (0, 1) if s % 2 == 0 else (2, 3))
+            if odd and c + 2 < BLOCKS:
+                x_quantise(c + 2)
+            if odd and c + 1 < BLOCKS:
+                g_quantise(c + 1)
+            if not odd and c + 2 < BLOCKS:
+                x_interleave(c + 2)
+            if c + 3 < BLOCKS:
+                widen(c + 3, (2, 3) if odd else (0, 1))
             for w in products[s]:
-                product(w)
-                finish(w)
-        for w in products[STEPS]:
-            product(w)
-            finish(w)
-        for name, w in roots[STEPS]:
+                product(nc.vector, w)
+            for w in products[s]:
+                finish(nc.gpsimd if s < STEPS - TAIL_V else nc.vector, w)
+        done = [w for group in products for w in group]
+        for name, w in last_roots:
             root(name, w)
-        for w in products[STEPS + 1]:
-            product(w)
-            finish(w)
+        for w in range(STEPS):
+            if w not in done:
+                product(nc.vector, w)
+                finish(nc.vector, w)

@@ -12,10 +12,10 @@ ROWS = 2 * P
 STEPS = N // ROWS
 CHUNK = 2 * ROWS
 BLOCKS = N // CHUNK
-GROUPS = [2, 4, 4, 4, 4, 4, 2]
+GROUPS = [3, 3, 3, 3, 3, 3, 2, 2, 2]
 S_INT = ()
 G_INT = (2, 3)
-TAIL_V = 1
+TAIL_V = 2
 ACT_RATE = (2, 3)
 ACT_LATE = 18
 LATE = 22
@@ -253,6 +253,7 @@ def tile_seminmfsquarerootupdate_t_kernel(tc, x_bytes, x_scale, f, g, m, c, d, o
             a_bank.append(t)
         g_scale(1)
         g_turn(2)
+        g_turn(3)
         widen(0, range(T))
         x_interleave(0)
         g_quantise(0)
@@ -280,9 +281,9 @@ def tile_seminmfsquarerootupdate_t_kernel(tc, x_bytes, x_scale, f, g, m, c, d, o
         nc.vector.tensor_copy(out=ap_i[:].rearrange("p (b i) t -> p b t i", i=4),
                               in_=ap_raw[:].rearrange("p t (b i) -> p b t i", i=4))
         anq = quantised(an_i, keep, "an", 1)
-        x_quantise(1)
+        g_scale(2)
         apq = quantised(ap_i, keep, "ap", 1)
-        widen(2, range(T))
+        widen(2, range(2))
 
         roots, products, last_roots = plan()
         for s in range(STEPS):
@@ -292,8 +293,8 @@ def tile_seminmfsquarerootupdate_t_kernel(tc, x_bytes, x_scale, f, g, m, c, d, o
             if s + 1 < STEPS:
                 p_matmul(2 * s + 2)
                 p_matmul(2 * s + 3)
-            if s + 3 < STEPS:
-                g_turn(s + 3)
+            if s + 4 < STEPS:
+                g_turn(s + 4)
             for name, w in roots[s][:1]:
                 root(name, w)
             if s + 1 < STEPS:
@@ -303,16 +304,16 @@ def tile_seminmfsquarerootupdate_t_kernel(tc, x_bytes, x_scale, f, g, m, c, d, o
                 root(name, w)
             ratio_parts(2 * s)
             ratio_parts(2 * s + 1)
-            if s + 2 < STEPS:
-                g_scale(s + 2)
+            if s + 3 < STEPS:
+                g_scale(s + 3)
             if odd and c + 2 < BLOCKS:
-                x_quantise(c + 2)
-            if odd and c + 1 < BLOCKS:
-                g_quantise(c + 1)
-            if not odd and c + 2 < BLOCKS:
                 x_interleave(c + 2)
-            if c + 3 < BLOCKS:
-                widen(c + 3, (2, 3) if odd else (0, 1))
+            if not odd and c + 1 < BLOCKS:
+                x_quantise(c + 1)
+                g_quantise(c + 1)
+            k = (s + 5) // 2
+            if k < BLOCKS:
+                widen(k, (0, 1) if odd else (2, 3))
             for w in products[s]:
                 product(nc.vector, w)
             for w in products[s]:

@@ -14,6 +14,7 @@ CHUNK = 2 * ROWS
 BLOCKS = N // CHUNK
 GROUPS = [3, 3, 3, 3, 3, 3, 2, 2, 2]
 S_INT = ()
+V_WIDEN = (1, 2, 3, 4)
 G_INT = (2, 3)
 TAIL_V = 2
 ACT_RATE = (2, 3)
@@ -134,8 +135,12 @@ def tile_seminmfsquarerootupdate_t_kernel(tc, x_bytes, x_scale, f, g, m, c, d, o
                 xw[k] = work.tile([P, T, CHUNK], BF16, name="xw", tag="raw", bufs=3)
             src, first = x_in[k]
             for t in planes:
-                nc.scalar.activation(xw[k][:, t, :], src[:, t, first:first + CHUNK].bitcast(FP8), ACT.Copy,
-                                     scale=xs_col[:, t:t + 1])
+                codes = src[:, t, first:first + CHUNK].bitcast(FP8)
+                if t == 3 and k in V_WIDEN:
+                    nc.vector.tensor_scalar(out=xw[k][:, t, :], in0=codes, scalar1=xs_col[:, t:t + 1],
+                                            scalar2=None, op0=ALU.mult)
+                else:
+                    nc.scalar.activation(xw[k][:, t, :], codes, ACT.Copy, scale=xs_col[:, t:t + 1])
 
         def x_interleave(k):
             xi[k] = work.tile([P, CHUNK, T], BF16, name="xi", tag="xi", bufs=3, align_bytes=64)
@@ -201,29 +206,33 @@ def tile_seminmfsquarerootupdate_t_kernel(tc, x_bytes, x_scale, f, g, m, c, d, o
 
         def ratio_parts(j):
             s, i = j // 2, j % 2
-            if i == 0:
+            if s not in num:
                 num[s] = work.tile([P, 2, R], F32, name="num", tag="num", bufs=NBUF)
                 den[s] = work.tile([P, 2, R], F32, name="den", tag="den", bufs=NBUF)
             nc.vector.scalar_tensor_tensor(
-                out=num[s][:, i, :], in0=pc[j][:], scalar=0.0, in1=nn[j][:], op0=ALU.max, op1=ALU.add)
-            nc.vector.scalar_tensor_tensor(
                 out=den[s][:, i, :], in0=pc[j][:], scalar=0.0, in1=dd[j][:], op0=ALU.min, op1=ALU.subtract)
+            nc.vector.scalar_tensor_tensor(
+                out=num[s][:, i, :], in0=pc[j][:], scalar=0.0, in1=nn[j][:], op0=ALU.max, op1=ALU.add)
 
-        def root(name, s):
+        def root(name, s, first=0, last=2):
             if name == "sqrt":
-                nc.scalar.activation(num[s][:], num[s][:], ACT.Sqrt)
+                nc.scalar.activation(num[s][:, first:last, :], num[s][:, first:last, :], ACT.Sqrt)
             else:
-                nc.scalar.activation(den[s][:], den[s][:], ACT.Abs_reciprocal_sqrt, scale=-1.0)
+                nc.scalar.activation(den[s][:, first:last, :], den[s][:, first:last, :], ACT.Abs_reciprocal_sqrt,
+                                     scale=-1.0)
 
-        def product(engine, s, first=0, last=2):
-            engine.tensor_tensor(out=num[s][:, first:last, :], in0=num[s][:, first:last, :],
-                                 in1=den[s][:, first:last, :], op=ALU.mult)
+        def product(s, first=0, last=2):
+            nc.vector.tensor_tensor(out=num[s][:, first:last, :], in0=num[s][:, first:last, :],
+                                    in1=den[s][:, first:last, :], op=ALU.mult)
 
-        def finish(engine, s):
-            src, first = g_in[s]
+        def finish(engine, s, first=0, last=2):
+            src, at = g_in[s]
             res = work.tile([P, 2, R], F32, name="res", tag="res", bufs=3)
-            engine.tensor_tensor(out=res[:], in0=num[s][:], in1=src[:, first:first + 2, :], op=ALU.mult)
-            nc.sync.dma_start(out=out[s * ROWS:(s + 1) * ROWS, :].rearrange("(i p) r -> p i r", p=P), in_=res[:])
+            engine.tensor_tensor(out=res[:, first:last, :], in0=num[s][:, first:last, :],
+                                 in1=src[:, at + first:at + last, :], op=ALU.mult)
+            rows = out[s * ROWS + first * P:s * ROWS + last * P, :].rearrange("(i p) r -> p i r", p=P)
+            nc.sync.dma_start(out=rows, in_=res[:, first:last, :])
+
 
         fm_raw = work.tile([P, T, R], BF16, name="fm_raw", tag="raw", bufs=3)
         for t in range(T):
@@ -288,8 +297,8 @@ def tile_seminmfsquarerootupdate_t_kernel(tc, x_bytes, x_scale, f, g, m, c, d, o
         roots, products, last_roots = plan()
         for s in range(STEPS):
             c, odd = s // 2, s % 2
-            g_matmul(2 * s)
             g_matmul(2 * s + 1)
+            g_matmul(2 * s)
             if s + 1 < STEPS:
                 p_matmul(2 * s + 2)
                 p_matmul(2 * s + 3)
@@ -302,8 +311,8 @@ def tile_seminmfsquarerootupdate_t_kernel(tc, x_bytes, x_scale, f, g, m, c, d, o
                 p_copy(2 * s + 3)
             for name, w in roots[s][1:]:
                 root(name, w)
-            ratio_parts(2 * s)
             ratio_parts(2 * s + 1)
+            ratio_parts(2 * s)
             if s + 3 < STEPS:
                 g_scale(s + 3)
             if odd and c + 2 < BLOCKS:
@@ -315,13 +324,17 @@ def tile_seminmfsquarerootupdate_t_kernel(tc, x_bytes, x_scale, f, g, m, c, d, o
             if k < BLOCKS:
                 widen(k, (0, 1) if odd else (2, 3))
             for w in products[s]:
-                product(nc.vector, w)
+                product(w)
             for w in products[s]:
                 finish(nc.gpsimd if s < STEPS - TAIL_V else nc.vector, w)
         done = [w for group in products for w in group]
-        for name, w in last_roots:
+        for name, w in last_roots[:-1]:
             root(name, w)
+        for i in range(2):
+            root(last_roots[-1][0], STEPS - 1, i, i + 1)
         for w in range(STEPS):
-            if w not in done:
-                product(nc.vector, w)
-                finish(nc.vector, w)
+            if w in done:
+                continue
+            for first, last in ((0, 1), (1, 2)) if w == STEPS - 1 else ((0, 2),):
+                product(w, first, last)
+                finish(nc.vector, w, first, last)

from contextlib import ExitStack

import concourse.mybir as mybir
from concourse.masks import make_identity

M, N, R = 512, 6144, 512
FLOPS = 2 * (3 * N * M * R + M * R * R)

P = 128
T = 4
ROWS = 2 * P
STEPS = N // ROWS
CHUNK = 2 * ROWS
BLOCKS = N // CHUNK
GROUPS = [3, 3, 3, 3, 3, 3, 2, 2, 2]
S_INT = ()
V_WIDEN = (1, 2, 3, 4)
G_INT = (2, 3)
TAIL_V = 2
ACT_RATE = (2, 3)
ACT_LATE = 18
LATE = 22
G_FIN = 2
NBUF = 9
G_HALF = False

F32 = mybir.dt.float32
BF16 = mybir.dt.bfloat16
U32 = mybir.dt.uint32
U8 = mybir.dt.uint8
FP8 = mybir.dt.float8_e4m3fn
FP8X4 = mybir.dt.float8_e4m3fn_x4
ALU = mybir.AluOpType
ACT = mybir.ActivationFunctionType

X_LOADS = [512, 512, 1024, 2048, 2048]
G_LOADS = [1, 1, 1, 1, 2, 2, 2, 2]


def plan():
    order = []
    first = 0
    for index, size in enumerate(GROUPS):
        names = ("sqrt", "rsqrt") if index % 2 == 0 else ("rsqrt", "sqrt")
        for name in names:
            for step in range(first, first + size):
                order.append((name, step))
        first += size
    roots, products = [], []
    seen = set()
    position = 0
    ready = []
    sent = 0
    for s in range(STEPS):
        count = min(len(ready) - sent, 1 if s < LATE else 2)
        products.append(ready[sent:sent + count])
        sent += count
        now = []
        while len(now) < ACT_RATE[s >= ACT_LATE] and position < len(order) and order[position][1] < s:
            name, step = order[position]
            now.append((name, step))
            if step in seen:
                ready.append(step)
            seen.add(step)
            position += 1
        roots.append(now)
    return roots, products, order[position:]


def tile_seminmfsquarerootupdate_t_kernel(tc, x_bytes, x_scale, f, g, m, c, d, out):
    nc = tc.nc
    with ExitStack() as ctx:
        keep = ctx.enter_context(tc.tile_pool(name="keep", bufs=1))
        work = ctx.enter_context(tc.tile_pool(name="work", bufs=2))
        psum = ctx.enter_context(tc.psum_pool(name="psum", bufs=2))
        ctx.enter_context(tc.manual_schedule())

        f_raw = work.tile([P, T, R], BF16, name="f_raw", tag="raw", bufs=3)
        f_rows = f.rearrange("(p t) r -> p t r", t=T)
        nc.sync.dma_start(out=f_raw[:, 0:2, :], in_=f_rows[:, 0:2, :])
        nc.sync.dma_start(out=f_raw[:, 2:4, :], in_=f_rows[:, 2:4, :])
        m_col = keep.tile([P, T], BF16, name="m_col")
        nc.scalar.dma_start(out=m_col[:], in_=m.rearrange("(p t) -> p t", t=T))
        xs_col = keep.tile([P, T], F32, name="xs_col")
        nc.scalar.dma_start(out=xs_col[:], in_=x_scale.rearrange("(p t) o -> p (t o)", t=T))
        c_col = keep.tile([P, T], BF16, name="c_col")
        nc.scalar.dma_start(out=c_col[:], in_=c.rearrange("(p t) -> p t", t=T))
        d_col = keep.tile([P, T], BF16, name="d_col")
        nc.scalar.dma_start(out=d_col[:], in_=d.rearrange("(p t) -> p t", t=T))

        xb = x_bytes.rearrange("(p t) n -> p t n", t=T)
        x_in = {}
        g_in = {}

        def load_x(index):
            first = sum(X_LOADS[:index])
            width = X_LOADS[index]
            t = keep.tile([P, T, width], U8, name="x_in%d" % index)
            nc.sync.dma_start(out=t[:], in_=xb[:, :, first:first + width])
            for k in range(width // CHUNK):
                x_in[first // CHUNK + k] = (t, k * CHUNK)

        def load_g(index):
            first = sum(G_LOADS[:index]) * CHUNK
            tiles = G_LOADS[index] * CHUNK // P
            t = keep.tile([P, tiles, R], BF16, name="g_in%d" % index)
            nc.sync.dma_start(out=t[:], in_=g[first:first + tiles * P, :].rearrange("(i p) r -> p i r", p=P))
            for k in range(tiles // 2):
                g_in[first // ROWS + k] = (t, 2 * k)

        load_x(0)
        load_g(0)
        load_x(1)
        load_g(1)
        load_x(2)
        load_g(2)
        load_g(3)
        load_x(3)
        load_g(4)
        load_g(5)
        load_x(4)
        load_g(6)
        load_g(7)

        ident = keep.tile([P, P], F32, name="ident")
        make_identity(nc, ident[:])

        xw, xi, xt, xq = {}, {}, {}, {}
        gt, gi, gq = {}, {}, {}
        pp, pc, nn, dd = {}, {}, {}, {}
        num, den = {}, {}

        def widen(k, planes):
            if k not in xw:
                xw[k] = work.tile([P, T, CHUNK], BF16, name="xw", tag="raw", bufs=3)
            src, first = x_in[k]
            for t in planes:
                codes = src[:, t, first:first + CHUNK].bitcast(FP8)
                if t == 3 and k in V_WIDEN:
                    nc.vector.tensor_scalar(out=xw[k][:, t, :], in0=codes, scalar1=xs_col[:, t:t + 1],
                                            scalar2=None, op0=ALU.mult)
                else:
                    nc.scalar.activation(xw[k][:, t, :], codes, ACT.Copy, scale=xs_col[:, t:t + 1])

        def x_interleave(k):
            xi[k] = work.tile([P, CHUNK, T], BF16, name="xi", tag="xi", bufs=3, align_bytes=64)
            if k in G_INT:
                nc.gpsimd.tensor_scalar(out=xi[k][:].rearrange("p (b i) t -> p b t i", i=4),
                                        in0=xw[k][:].rearrange("p t (b i) -> p b t i", i=4),
                                        scalar1=1.0, scalar2=0.0, op0=ALU.mult, op1=ALU.add)
                return
            engine = nc.scalar.copy if k in S_INT else nc.vector.tensor_copy
            engine(out=xi[k][:].rearrange("p (b i) t -> p b t i", i=4),
                   in_=xw[k][:].rearrange("p t (b i) -> p b t i", i=4))

        def g_turn(s):
            src, first = g_in[s]
            gt[s] = psum.tile([P, 2, ROWS], F32, name="gt", tag="gt", bufs=2)
            for u in range(2):
                for i in range(2):
                    words = src[:, first + i, :].bitcast(F32)
                    nc.tensor.transpose(gt[s][:, u, i * P:(i + 1) * P], words[:, u::2], ident[:])

        def g_scale(s):
            k, h = s // 2, s % 2
            if h == 0:
                gi[k] = work.tile([P, CHUNK, T], BF16, name="gi", tag="il", bufs=3, align_bytes=64)
            nc.vector.tensor_tensor(
                out=gi[k][:, h * ROWS:(h + 1) * ROWS, :].rearrange("p n (u e) -> p n u e", e=2),
                in0=gt[s][:].bitcast(BF16).rearrange("p u (n e) -> p n u e", e=2),
                in1=c_col[:].rearrange("p (u e) -> p u e", e=2).unsqueeze(1).to_broadcast([P, ROWS, 2, 2]),
                op=ALU.mult)

        def quantised(src, pool, tag, bufs):
            codes = pool.tile([P, CHUNK], U32, name=tag + "_codes", tag=tag + "_codes", bufs=bufs, align_bytes=64)
            scales = pool.tile([P, CHUNK], U8, name=tag + "_scales", tag=tag + "_scales", bufs=bufs, align_bytes=64)
            nc.vector.quantize_mx(out=codes[:].bitcast(FP8X4), scales=scales[:],
                                  in_=src[:].rearrange("p n t -> p (n t)"))
            return codes, scales

        def x_quantise(k):
            xq[k] = quantised(xi[k], work, "xq", 3)

        def g_quantise(k):
            gq[k] = quantised(gi[k], work, "gq", 3)

        def mm(dst, stationary, first, moving):
            nc.tensor.matmul_mx(
                out=dst, lhsT=stationary[0][:, first:first + P].bitcast(FP8X4),
                lhsT_scale=stationary[1][:, first:first + P],
                rhs=moving[0][:].bitcast(FP8X4), rhs_scale=moving[1][:], start=True, stop=True)

        def p_matmul(j):
            pp[j] = psum.tile([P, R], F32, name="pp", tag="pp", bufs=2)
            mm(pp[j][:], xq[j // 4], (j % 4) * P, fmq)

        def p_copy(j):
            pc[j] = work.tile([P, R], F32, name="pc", tag="pc", bufs=8)
            nc.scalar.copy(out=pc[j][:], in_=pp[j][:])

        def g_matmul(j):
            nn[j] = psum.tile([P, R], F32, name="nn", tag="nn", bufs=2)
            mm(nn[j][:], gq[j // 4], (j % 4) * P, anq)
            dd[j] = psum.tile([P, R], F32, name="dd", tag="dd", bufs=2)
            mm(dd[j][:], gq[j // 4], (j % 4) * P, apq)

        def ratio_parts(j):
            s, i = j // 2, j % 2
            if s not in num:
                num[s] = work.tile([P, 2, R], F32, name="num", tag="num", bufs=NBUF)
                den[s] = work.tile([P, 2, R], F32, name="den", tag="den", bufs=NBUF)
            nc.vector.scalar_tensor_tensor(
                out=den[s][:, i, :], in0=pc[j][:], scalar=0.0, in1=dd[j][:], op0=ALU.min, op1=ALU.subtract)
            nc.vector.scalar_tensor_tensor(
                out=num[s][:, i, :], in0=pc[j][:], scalar=0.0, in1=nn[j][:], op0=ALU.max, op1=ALU.add)

        def root(name, s, first=0, last=2):
            if name == "sqrt":
                nc.scalar.activation(num[s][:, first:last, :], num[s][:, first:last, :], ACT.Sqrt)
            else:
                nc.scalar.activation(den[s][:, first:last, :], den[s][:, first:last, :], ACT.Abs_reciprocal_sqrt,
                                     scale=-1.0)

        def product(s, first=0, last=2):
            nc.vector.tensor_tensor(out=num[s][:, first:last, :], in0=num[s][:, first:last, :],
                                    in1=den[s][:, first:last, :], op=ALU.mult)

        def finish(engine, s, first=0, last=2):
            src, at = g_in[s]
            res = work.tile([P, 2, R], F32, name="res", tag="res", bufs=3)
            engine.tensor_tensor(out=res[:, first:last, :], in0=num[s][:, first:last, :],
                                 in1=src[:, at + first:at + last, :], op=ALU.mult)
            rows = out[s * ROWS + first * P:s * ROWS + last * P, :].rearrange("(i p) r -> p i r", p=P)
            nc.sync.dma_start(out=rows, in_=res[:, first:last, :])


        fm_raw = work.tile([P, T, R], BF16, name="fm_raw", tag="raw", bufs=3)
        for t in range(T):
            nc.vector.tensor_scalar(out=fm_raw[:, t, :], in0=f_raw[:, t, :], scalar1=m_col[:, t:t + 1],
                                    scalar2=None, op0=ALU.mult)
        fi = work.tile([P, R, T], BF16, name="fi", tag="il", bufs=3, align_bytes=64)
        nc.scalar.copy(out=fi[:].rearrange("p (q w) t -> p q w t", q=T),
                       in_=f_raw[:].rearrange("p t (w q) -> p q w t", q=T))
        fmi = work.tile([P, R, T], BF16, name="fmi", tag="il", bufs=3, align_bytes=64)
        nc.vector.tensor_copy(out=fmi[:].rearrange("p (b i) t -> p b t i", i=4),
                              in_=fm_raw[:].rearrange("p t (b i) -> p b t i", i=4))
        e_col = keep.tile([P, T], F32, name="e_col")
        nc.vector.tensor_tensor(out=e_col[:], in0=c_col[:], in1=d_col[:], op=ALU.mult)
        ne_col = keep.tile([P, T], F32, name="ne_col")
        nc.vector.tensor_scalar(out=ne_col[:], in0=e_col[:], scalar1=-1.0, scalar2=None, op0=ALU.mult)

        g_turn(0)
        g_turn(1)
        g_scale(0)
        fmq = quantised(fmi, keep, "fm", 1)
        fq = quantised(fi, keep, "f", 1)
        a_tags = ("nn", "dd", "nn", "dd")
        a_bank = []
        for q in range(T):
            t = psum.tile([P, R], F32, name="a%d" % q, tag=a_tags[q], bufs=2)
            mm(t[:], fq, q * P, fmq)
            a_bank.append(t)
        g_scale(1)
        g_turn(2)
        g_turn(3)
        widen(0, range(T))
        x_interleave(0)
        g_quantise(0)
        a_sb = [work.tile([P, 2, R], F32, name="a_sb%d" % h, tag="num", bufs=NBUF) for h in range(2)]
        for q in range(T):
            nc.scalar.copy(out=a_sb[q // 2][:, q % 2, :], in_=a_bank[q][:])
        x_quantise(0)
        widen(1, range(T))
        an_raw = work.tile([P, T, R], BF16, name="an_raw", tag="raw", bufs=3)
        for q in range(T):
            nc.vector.tensor_scalar(out=an_raw[:, q, :], in0=a_sb[q // 2][:, q % 2, :], scalar1=0.0,
                                    scalar2=ne_col[:, q:q + 1], op0=ALU.min, op1=ALU.mult)
        an_i = work.tile([P, R, T], BF16, name="an_i", tag="il", bufs=3, align_bytes=64)
        nc.scalar.copy(out=an_i[:].rearrange("p (b i) t -> p b t i", i=4),
                       in_=an_raw[:].rearrange("p t (b i) -> p b t i", i=4))
        ap_raw = work.tile([P, T, R], BF16, name="ap_raw", tag="raw", bufs=3)
        for q in range(T):
            nc.vector.tensor_scalar(out=ap_raw[:, q, :], in0=a_sb[q // 2][:, q % 2, :], scalar1=0.0,
                                    scalar2=e_col[:, q:q + 1], op0=ALU.max, op1=ALU.mult)
        x_interleave(1)
        for j in range(2):
            p_matmul(j)
            p_copy(j)
        ap_i = work.tile([P, R, T], BF16, name="ap_i", tag="il", bufs=3, align_bytes=64)
        nc.vector.tensor_copy(out=ap_i[:].rearrange("p (b i) t -> p b t i", i=4),
                              in_=ap_raw[:].rearrange("p t (b i) -> p b t i", i=4))
        anq = quantised(an_i, keep, "an", 1)
        g_scale(2)
        apq = quantised(ap_i, keep, "ap", 1)
        widen(2, range(2))

        roots, products, last_roots = plan()
        for s in range(STEPS):
            c, odd = s // 2, s % 2
            g_matmul(2 * s + 1)
            g_matmul(2 * s)
            if s + 1 < STEPS:
                p_matmul(2 * s + 2)
                p_matmul(2 * s + 3)
            if s + 4 < STEPS:
                g_turn(s + 4)
            for name, w in roots[s][:1]:
                root(name, w)
            if s + 1 < STEPS:
                p_copy(2 * s + 2)
                p_copy(2 * s + 3)
            for name, w in roots[s][1:]:
                root(name, w)
            ratio_parts(2 * s + 1)
            ratio_parts(2 * s)
            if s + 3 < STEPS:
                g_scale(s + 3)
            if odd and c + 2 < BLOCKS:
                x_interleave(c + 2)
            if not odd and c + 1 < BLOCKS:
                x_quantise(c + 1)
                g_quantise(c + 1)
            k = (s + 5) // 2
            if k < BLOCKS:
                widen(k, (0, 1) if odd else (2, 3))
            for w in products[s]:
                product(w)
            for w in products[s]:
                finish(nc.gpsimd if s < STEPS - TAIL_V else nc.vector, w)
        done = [w for group in products for w in group]
        for name, w in last_roots[:-1]:
            root(name, w)
        for i in range(2):
            root(last_roots[-1][0], STEPS - 1, i, i + 1)
        for w in range(STEPS):
            if w in done:
                continue
            for first, last in ((0, 1), (1, 2)) if w == STEPS - 1 else ((0, 2),):
                product(w, first, last)
                finish(nc.vector, w, first, last)
